import numpy as np
import ml_dtypes


def mxq(x, axis, fmt="e4m3"):
    dtype, down = {"e4m3": (ml_dtypes.float8_e4m3fn, 7), "e5m2": (ml_dtypes.float8_e5m2, 14)}[fmt]
    v = np.moveaxis(np.asarray(x, np.float32).astype(ml_dtypes.bfloat16).astype(np.float64), axis, -1)
    blocks = v.reshape(v.shape[:-1] + (-1, 32))
    amax = np.abs(blocks).max(-1, keepdims=True)
    byte = np.maximum(np.where(amax > 0, np.frexp(amax)[1] - 1 + 127, 0) - down, 1)
    scale = np.exp2(byte - 127.0)
    codes = (blocks / scale).astype(np.float32).astype(dtype).astype(np.float64)
    return np.moveaxis((codes * scale).reshape(v.shape), -1, axis)


WIDE = False


def mx_kscale(k):
    if not WIDE:
        return np.ones(k)
    levels = np.array([24, -24, 12, -12, 0])
    if k % 512:
        return np.exp2(np.random.permutation(np.resize(levels, k // 32))).repeat(32)
    a = np.empty((k // 512, 16))
    for p in range(k // 512):
        a[p, :8] = np.random.permutation(np.resize(levels, 8))
        for g in range(8):
            far = levels[np.abs(levels - a[p, g]) >= 10]
            a[p, g + 8] = far[np.random.randint(len(far))]
    return np.exp2(a.ravel()).repeat(32)


def f64(x):
    return np.asarray(x).astype(np.float64)


def striped(idx):
    return np.tile(idx.reshape(-1, 16).T, (8, 1)).astype(np.uint16)


def unstriped(offs):
    return offs[:16].T.reshape(-1).astype(np.int64)


E2M1 = np.array([0.0, 0.5, 1.0, 1.5, 2.0, 3.0, 4.0, 6.0, -0.0, -0.5, -1.0, -1.5, -2.0, -3.0, -4.0, -6.0])


def pack_weight(w, fmt):
    k, n = w.shape
    w = f64(np.asarray(w, np.float32).astype(ml_dtypes.bfloat16)).reshape(k // 32, 32, n)
    amax = np.abs(w).max(1)
    if fmt == "e4m3":
        byte = np.frexp(amax)[1] - 1 + 127 - 7
    else:
        mant, ex = np.frexp(amax / 6.0)
        byte = np.where(mant > 0.5, ex, ex - 1) + 127
    byte = np.clip(np.where(amax > 0, byte, 1), 1, 254)
    scaled = (w * np.exp2(127.0 - byte)[:, None, :]).reshape(k, n).astype(np.float32)
    by_word = np.ascontiguousarray(scaled.reshape(k // 512, 128, 4, n).transpose(0, 1, 3, 2))
    if fmt == "e4m3":
        words = by_word.astype(ml_dtypes.float8_e4m3fn).view(np.uint8)
    else:
        c = by_word.astype(ml_dtypes.float4_e2m1fn).view(np.uint8) & 0xF
        words = (c[..., 0::2] | (c[..., 1::2] << 4)).reshape(k // 512, 128, 2 * n)
    return np.ascontiguousarray(words), np.ascontiguousarray(byte.astype(np.uint8).reshape(k // 512, 16, n))


def unpack_weight(words, scales, fmt):
    g, _, n = scales.shape
    words = np.ascontiguousarray(words).reshape(g, 128, n, -1)
    if fmt == "e4m3":
        vals = words.view(ml_dtypes.float8_e4m3fn).astype(np.float64)
    else:
        nib = np.empty((g, 128, n, 4), np.uint8)
        nib[..., 0::2] = words & 0xF
        nib[..., 1::2] = words >> 4
        vals = E2M1[nib]
    vals = vals * np.repeat(np.exp2(scales.astype(np.float64) - 127.0), 8, axis=1)[..., None]
    return vals.transpose(0, 1, 3, 2).reshape(g * 512, n)


def pack_table4(v):
    words, scales = pack_weight(v, "e2m1")
    g, t = words.shape[0] // 2, v.shape[1]
    return np.ascontiguousarray(words.reshape(g, 2, 128, t, 2).transpose(0, 2, 3, 1, 4).reshape(g, 128, t, 4)), scales


def unpack_table4(words, scales):
    g, _, t, _ = words.shape
    return unpack_weight(words.reshape(g, 128, t, 2, 2).transpose(0, 3, 1, 2, 4).reshape(2 * g, 128, 2 * t), scales, "e2m1")


def sigm(f):
    return 1.0 / (1.0 + np.exp(-np.maximum(f, -700.0)))


K, R, N, T, J = 1024, 512, 512, 2048, 1024


def setup_inputs():
    n = np.random.standard_normal
    s = mx_kscale(K)[:, None]
    u = mx_kscale(R)[:, None]
    p_tab = pack_table4(n((K, T)) * s)
    p_wu = pack_weight(n((K, R)) / np.sqrt(K) / s * u.T, "e4m3")
    p_wd = pack_weight(n((R, N)) / np.sqrt(R) / u, "e2m1")
    return {
        "tab_words": p_tab[0],
        "tab_scales": p_tab[1],
        "wg": (n((K, R)) / np.sqrt(K) / s).astype(np.float32),
        "wu_words": p_wu[0],
        "wu_scales": p_wu[1],
        "wd_words": p_wd[0],
        "wd_scales": p_wd[1],
        "b": (0.3 * n(N)).astype(np.float32),
        "offs": striped(np.random.permutation(T)[:J]),
    }


def reference(tab_words, tab_scales, wg, wu_words, wu_scales, wd_words, wd_scales, b, offs):
    idx = unstriped(offs)
    tab_ = unpack_table4(tab_words, tab_scales)[:, idx]
    wg_ = mxq(f64(wg), 0, "e4m3")
    wu_ = unpack_weight(wu_words, wu_scales, "e4m3")
    ga = wg_.T @ tab_
    ub = wu_.T @ tab_
    h = sigm(ga) * ub
    h_ = mxq(h, 0, "e4m3")
    wd_ = unpack_weight(wd_words, wd_scales, "e2m1")
    y = wd_.T @ h_
    return y + f64(b)[:, None]

@@ -1,0 +1,249 @@
+from contextlib import ExitStack
+
+import concourse.mybir as mybir
+
+K, R, N, T, J = 1024, 512, 512, 2048, 1024
+FLOPS = 2 * J * (2 * K * R + R * N)
+
+F32 = mybir.dt.float32
+BF16 = mybir.dt.bfloat16
+I32 = mybir.dt.int32
+U32 = mybir.dt.uint32
+U16 = mybir.dt.uint16
+U8 = mybir.dt.uint8
+FP8X4 = mybir.dt.float8_e4m3fn_x4
+FP4X4 = mybir.dt.float4_e2m1fn_x4
+ACT = mybir.ActivationFunctionType
+ALU = mybir.AluOpType
+
+P = 128
+PACK = 4
+PASSES = K // (P * PACK)
+CHUNK = 128
+GROUP = 256
+ROW0 = 96
+PIECES = ((0, 256), (256, 256), (512, 512))
+SCALAR_M = (96, 64)
+EARLY_UP = 6
+
+
+def tile_list_gmlpt_sigm_bias_kernel(
+    tc, tab_words, tab_scales, wg, wu_words, wu_scales, wd_words, wd_scales, b, offs, out
+):
+    nc = tc.nc
+    with ExitStack() as ctx:
+        keep = ctx.enter_context(tc.tile_pool(name="keep", bufs=1))
+        ring = ctx.enter_context(tc.tile_pool(name="ring", bufs=3))
+        psum = ctx.enter_context(tc.psum_pool(name="psum", bufs=1))
+
+        offsets = keep.tile([P, J // 16], U16, name="offsets")
+        nc.sync.dma_start(offsets[:], offs)
+
+        tab_sc = keep.tile([P, T], U8, name="tab_sc", align_bytes=64)
+        nc.sync.dma_start(tab_sc[ROW0:P, :].bitcast(I32), tab_scales.rearrange("a q t -> (a q) t").bitcast(I32))
+        wu_sc_raw = keep.tile([P, R], U8, name="wu_sc_raw", align_bytes=64)
+        nc.scalar.dma_start(wu_sc_raw[ROW0:P, :].bitcast(I32), wu_scales.rearrange("a q r -> (a q) r").bitcast(I32))
+        rows = keep.tile([P, J + R + N], U8, name="rows", align_bytes=64)
+        nc.scalar.dma_start(rows[ROW0 : ROW0 + 16, J + R :].bitcast(I32), wd_scales[0].bitcast(I32))
+        wu_raw = keep.tile([P, PASSES, R], I32, name="wu_raw", align_bytes=64)
+        nc.sync.dma_start(wu_raw[:], wu_words.rearrange("a p r i -> p a (r i)").bitcast(I32))
+        tab = keep.tile([P, T], I32, name="tab", align_bytes=64)
+        nc.sync.dma_start(tab[:], tab_words[0].rearrange("p t i -> p (t i)").bitcast(I32))
+        wg_raw = []
+        for a in range(PASSES):
+            raw = keep.tile([P, PACK, R], F32, name=f"wg_raw{a}", tag=f"stage{a}", align_bytes=64)
+            nc.sync.dma_start(raw[:], wg[512 * a : 512 * (a + 1), :].rearrange("(p i) r -> p i r", i=PACK))
+            wg_raw.append(raw)
+
+        nc.vector.memset(tab_sc[0:ROW0, :].bitcast(I32), 0)
+        nc.vector.memset(wu_sc_raw[0:ROW0, :].bitcast(I32), 0)
+        warm = keep.tile([P, 2], F32, name="warm")
+        nc.vector.memset(warm[:, 0:1], 0.0)
+        nc.scalar.activation(warm[:, 1:2], warm[:, 0:1], ACT.Sigmoid)
+        widths = (J + R + N, J + R)
+        planes = []
+        for a in range(PASSES):
+            plane = keep.tile([P, widths[a]], U8, name=f"plane{a}", align_bytes=64)
+            nc.vector.memset(plane[:].bitcast(I32), 0)
+            planes.append(plane)
+
+        picked_sc = keep.tile([P, J], U8, name="picked_sc", align_bytes=64)
+        nc.vector.tensor_copy(picked_sc[:], tab_sc[:].indirect(offsets[:]))
+        nc.vector.tensor_copy(
+            rows[:, J : J + R].rearrange("p (t m) -> p t m", t=PACK),
+            wu_sc_raw[:].rearrange("p (m t) -> p t m", t=PACK),
+        )
+        nc.vector.tensor_copy(rows[ROW0:P, 0:J].bitcast(I32), picked_sc[ROW0:P, :].bitcast(I32))
+        for a in range(PASSES):
+            for q in range(4):
+                eng = nc.gpsimd if (a == 1 and q >= 2) else nc.scalar
+                src = ROW0 + 16 * a + 4 * q
+                eng.dma_start(
+                    planes[a][32 * q : 32 * q + 4, :].bitcast(I32),
+                    rows[src : src + 4, 0 : widths[a]].bitcast(I32),
+                )
+
+        wu_codes = keep.tile([P, PASSES, R], I32, name="wu_codes", align_bytes=64)
+        for a in range(PASSES):
+            nc.vector.tensor_copy(
+                wu_codes[:, a, :].rearrange("p (t m) -> p m t", t=PACK),
+                wu_raw[:, a, :].rearrange("p (m t) -> p m t", t=PACK),
+            )
+
+        moving = {}
+        for j0, n in PIECES:
+            both = keep.tile([P, n], U32, name=f"both{j0}", align_bytes=64)
+            nc.vector.tensor_copy(both[:], tab[:].bitcast(U32).indirect(offsets[:, j0 // 16 : (j0 + n) // 16]))
+            parted = keep.tile([P, PASSES, n], U16, name=f"parted{j0}", align_bytes=64)
+            nc.vector.tensor_copy(parted[:], both[:].bitcast(U16).rearrange("p (j a) -> p a j", a=PASSES))
+            for c in range(j0 // CHUNK, (j0 + n) // CHUNK):
+                for a in range(PASSES):
+                    moving[c, a] = parted[:, a, c * CHUNK - j0 : (c + 1) * CHUNK - j0].bitcast(FP4X4)
+
+        def bank(i, name):
+            return psum.tile([P, 512], F32, name=name, tag=f"bank{i}")
+
+        def first_stage(acc, codes, scales, c, a):
+            for t in range(PACK):
+                nc.tensor.matmul_mx(
+                    out=acc[:, t * CHUNK : (t + 1) * CHUNK],
+                    lhsT=codes[:, t * P : (t + 1) * P].bitcast(FP8X4),
+                    lhsT_scale=scales[:, t * P : (t + 1) * P],
+                    rhs=moving[c, a],
+                    rhs_scale=planes[a][:, c * CHUNK : (c + 1) * CHUNK],
+                    start=(a == 0 and t == 0),
+                    stop=(a == PASSES - 1 and t == PACK - 1),
+                )
+
+        up, gate = {}, {}
+
+        def up_pass(c, a):
+            first_stage(up[c], wu_codes[:, a, :], planes[a][:, J : J + R], c, a)
+
+        def gate_pass(c, a):
+            first_stage(gate[c], wg_codes[a], wg_sc[a], c, a)
+
+        for c in range(EARLY_UP):
+            up[c] = bank(c, f"up{c}")
+        for c in range(4):
+            up_pass(c, 0)
+        for c in range(4):
+            up_pass(c, 1)
+        for c in range(4, EARLY_UP):
+            up_pass(c, 0)
+            up_pass(c, 1)
+
+        wg_codes, wg_sc = [], []
+        for a in range(PASSES):
+            woven = keep.tile([P, PACK * R], BF16, name=f"wg_woven{a}", align_bytes=64)
+            dst = woven[:].rearrange("p (t m i) -> p m t i", t=PACK, i=PACK)
+            src = wg_raw[a][:].rearrange("p i (m t) -> p m t i", t=PACK)
+            cut = SCALAR_M[a]
+            nc.scalar.copy(dst[:, 0:cut], src[:, 0:cut])
+            nc.vector.tensor_copy(dst[:, cut:P], src[:, cut:P])
+            codes = keep.tile([P, R], U32, name=f"wg_codes{a}", align_bytes=64)
+            scales = keep.tile([P, R], U8, name=f"wg_sc{a}", align_bytes=64)
+            nc.vector.quantize_mx(out=codes[:].bitcast(FP8X4), scales=scales[:], in_=woven[:])
+            wg_codes.append(codes[:])
+            wg_sc.append(scales[:])
+
+        wd = keep.tile([P, 2 * N], U8, name="wd", tag="stage0", align_bytes=64)
+        nc.sync.dma_start(wd[:].bitcast(I32), wd_words[0].bitcast(I32))
+        bias = keep.tile([P, N // P], F32, name="bias", tag="stage1", align_bytes=64)
+        with nc.allow_non_contiguous_dma(reason="one bias value a partition and row tile"):
+            nc.sync.dma_start(bias[:], b.rearrange("(i p) -> p i", p=P))
+
+        hidden, quantised = {}, {}
+
+        def sigmoid(c):
+            s = ring.tile([P, CHUNK, PACK], F32, name="sig")
+            nc.scalar.activation(s[:], gate[c][:].rearrange("p (t j) -> p j t", t=PACK), ACT.Sigmoid)
+            return s
+
+        def product(c, s):
+            g, half = divmod(c, GROUP // CHUNK)
+            if half == 0:
+                hidden[g] = ring.tile([P, GROUP, PACK], BF16, name="hidden", align_bytes=64)
+            nc.vector.tensor_tensor(
+                hidden[g][:, half * CHUNK : (half + 1) * CHUNK, :],
+                up[c][:].rearrange("p (t j) -> p j t", t=PACK),
+                s[:],
+                ALU.mult,
+            )
+
+        def quantise(g):
+            codes = ring.tile([P, GROUP], U32, name="h_codes", align_bytes=64)
+            scales = ring.tile([P, GROUP], U8, name="h_sc", align_bytes=64)
+            nc.vector.quantize_mx(
+                out=codes[:].bitcast(FP8X4), scales=scales[:], in_=hidden[g][:].rearrange("p j t -> p (j t)")
+            )
+            quantised[g] = (codes, scales)
+
+        out_tiles = out.rearrange("(i p) j -> p i j", p=P)
+
+        def second_stage(g, banks):
+            codes, scales = quantised[g]
+            for pair in range(2):
+                acc = bank(banks[pair], f"down{g}_{pair}")
+                res = ring.tile([P, 2, GROUP], F32, name=f"res{pair}")
+                for e in range(2):
+                    i = 2 * pair + e
+                    nc.tensor.matmul_mx(
+                        out=acc[:, e * GROUP : (e + 1) * GROUP],
+                        lhsT=wd[:, 2 * P * i : 2 * P * (i + 1)].bitcast(FP4X4),
+                        lhsT_scale=planes[0][:, J + R + P * i : J + R + P * (i + 1)],
+                        rhs=codes[:].bitcast(FP8X4),
+                        rhs_scale=scales[:],
+                        start=True,
+                        stop=True,
+                    )
+                for e in range(2):
+                    i = 2 * pair + e
+                    if pair == 0 or g == 0:
+                        nc.scalar.activation(
+                            res[:, e, :], acc[:, e * GROUP : (e + 1) * GROUP], ACT.Identity, bias=bias[:, i : i + 1]
+                        )
+                    else:
+                        nc.vector.tensor_scalar_add(res[:, e, :], acc[:, e * GROUP : (e + 1) * GROUP], bias[:, i : i + 1])
+                nc.sync.dma_start(out_tiles[:, 2 * pair : 2 * pair + 2, g * GROUP : (g + 1) * GROUP], res[:])
+
+        sigs = {}
+
+        def gate_chunk(c, passes):
+            if 0 in passes:
+                gate[c] = bank(6 + c % 2, f"gate{c}")
+            for a in passes:
+                gate_pass(c, a)
+            if 1 in passes:
+                sigs[c] = sigmoid(c)
+
+        gate_chunk(0, (0,))
+        gate_chunk(1, (0,))
+        gate_chunk(0, (1,))
+        gate_chunk(1, (1,))
+        product(0, sigs[0])
+        gate_chunk(2, (0, 1))
+        product(1, sigs[1])
+        gate_chunk(3, (0, 1))
+        product(2, sigs[2])
+        quantise(0)
+        second_stage(0, (0, 1))
+        gate_chunk(4, (0, 1))
+        product(3, sigs[3])
+        gate_chunk(5, (0, 1))
+        product(4, sigs[4])
+        quantise(1)
+        second_stage(1, (0, 1))
+        gate_chunk(6, (0, 1))
+        product(5, sigs[5])
+        gate_chunk(7, (0, 1))
+        for c in (6, 7):
+            up[c] = bank(c - 4, f"up{c}")
+            up_pass(c, 0)
+            up_pass(c, 1)
+        quantise(2)
+        product(6, sigs[6])
+        product(7, sigs[7])
+        second_stage(2, (4, 5))
+        quantise(3)
+        second_stage(3, (0, 1))

@@ -20,11 +20,12 @@ P = 128
 PACK = 4
 PASSES = K // (P * PACK)
 CHUNK = 128
-GROUP = 256
-ROW0 = 96
-PIECES = ((0, 256), (256, 256), (512, 512))
-SCALAR_M = (96, 64)
+SCALAR_M = (128, 44)
+GROUPS = ((0, 1), (2, 3), (4, 5), (6,), (7,))
 EARLY_UP = 6
+SCALAR_GROUPS = (1, 2)
+GATE_BANKS = (6, 7, 0, 1)
+BOTH_TAGS = {0: "both0", 256: "both256", 512: "wu_raw1", 768: "woven1"}
 
 
 def tile_list_gmlpt_sigm_bias_kernel(
@@ -33,66 +34,64 @@ def tile_list_gmlpt_sigm_bias_kernel(
     nc = tc.nc
     with ExitStack() as ctx:
         keep = ctx.enter_context(tc.tile_pool(name="keep", bufs=1))
-        ring = ctx.enter_context(tc.tile_pool(name="ring", bufs=3))
+        ring = ctx.enter_context(tc.tile_pool(name="ring", bufs=4))
         psum = ctx.enter_context(tc.psum_pool(name="psum", bufs=1))
 
         offsets = keep.tile([P, J // 16], U16, name="offsets")
         nc.sync.dma_start(offsets[:], offs)
 
-        tab_sc = keep.tile([P, T], U8, name="tab_sc", align_bytes=64)
-        nc.sync.dma_start(tab_sc[ROW0:P, :].bitcast(I32), tab_scales.rearrange("a q t -> (a q) t").bitcast(I32))
-        wu_sc_raw = keep.tile([P, R], U8, name="wu_sc_raw", align_bytes=64)
-        nc.scalar.dma_start(wu_sc_raw[ROW0:P, :].bitcast(I32), wu_scales.rearrange("a q r -> (a q) r").bitcast(I32))
-        rows = keep.tile([P, J + R + N], U8, name="rows", align_bytes=64)
-        nc.scalar.dma_start(rows[ROW0 : ROW0 + 16, J + R :].bitcast(I32), wd_scales[0].bitcast(I32))
-        wu_raw = keep.tile([P, PASSES, R], I32, name="wu_raw", align_bytes=64)
-        nc.sync.dma_start(wu_raw[:], wu_words.rearrange("a p r i -> p a (r i)").bitcast(I32))
-        tab = keep.tile([P, T], I32, name="tab", align_bytes=64)
-        nc.sync.dma_start(tab[:], tab_words[0].rearrange("p t i -> p (t i)").bitcast(I32))
-        wg_raw = []
-        for a in range(PASSES):
+        def load_up_words(a):
+            raw = keep.tile([P, R], I32, name=f"wu_raw{a}", tag=f"wu_raw{a}", align_bytes=64)
+            nc.sync.dma_start(raw[:], wu_words[a].rearrange("p r i -> p (r i)").bitcast(I32))
+            return raw
+
+        def load_gate_rows(a):
             raw = keep.tile([P, PACK, R], F32, name=f"wg_raw{a}", tag=f"stage{a}", align_bytes=64)
             nc.sync.dma_start(raw[:], wg[512 * a : 512 * (a + 1), :].rearrange("(p i) r -> p i r", i=PACK))
-            wg_raw.append(raw)
+            return raw
 
-        nc.vector.memset(tab_sc[0:ROW0, :].bitcast(I32), 0)
-        nc.vector.memset(wu_sc_raw[0:ROW0, :].bitcast(I32), 0)
+        wu_raw = [load_up_words(0)]
+        tab_sc = keep.tile([P, T], U8, name="tab_sc", align_bytes=64)
+        nc.vector.memset(tab_sc[:].bitcast(I32), 0)
+        tab_rows = tab_scales.rearrange("a (q r) t -> r q a t", r=4).bitcast(I32)
+        for r in range(4):
+            nc.sync.dma_start(tab_sc[r:P:16, :].bitcast(I32), tab_rows[r])
+        tab = keep.tile([P, T], I32, name="tab", align_bytes=64)
+        nc.sync.dma_start(tab[:], tab_words[0].rearrange("p t i -> p (t i)").bitcast(I32))
+        wu_sc_raw = keep.tile([P, PASSES, R], U8, name="wu_sc_raw", tag="both256", align_bytes=64)
+        nc.vector.memset(wu_sc_raw[:].bitcast(I32), 0)
+        wu_rows = wu_scales.rearrange("a (q r) n -> q r a n", r=4).bitcast(I32)
+        for q in range(4):
+            nc.sync.dma_start(wu_sc_raw[32 * q : 32 * q + 4, :, :].bitcast(I32), wu_rows[q])
+        wu_raw.append(load_up_words(1))
+        wg_raw = [load_gate_rows(0)]
+
         warm = keep.tile([P, 2], F32, name="warm")
         nc.vector.memset(warm[:, 0:1], 0.0)
         nc.scalar.activation(warm[:, 1:2], warm[:, 0:1], ACT.Sigmoid)
-        widths = (J + R + N, J + R)
-        planes = []
-        for a in range(PASSES):
-            plane = keep.tile([P, widths[a]], U8, name=f"plane{a}", align_bytes=64)
-            nc.vector.memset(plane[:].bitcast(I32), 0)
-            planes.append(plane)
 
         picked_sc = keep.tile([P, J], U8, name="picked_sc", align_bytes=64)
+        moved_sc = keep.tile([P, J], U8, name="moved_sc", align_bytes=64)
+        nc.vector.memset(moved_sc[:].bitcast(I32), 0)
         nc.vector.tensor_copy(picked_sc[:], tab_sc[:].indirect(offsets[:]))
-        nc.vector.tensor_copy(
-            rows[:, J : J + R].rearrange("p (t m) -> p t m", t=PACK),
-            wu_sc_raw[:].rearrange("p (m t) -> p t m", t=PACK),
-        )
-        nc.vector.tensor_copy(rows[ROW0:P, 0:J].bitcast(I32), picked_sc[ROW0:P, :].bitcast(I32))
-        for a in range(PASSES):
-            for q in range(4):
-                eng = nc.gpsimd if (a == 1 and q >= 2) else nc.scalar
-                src = ROW0 + 16 * a + 4 * q
-                eng.dma_start(
-                    planes[a][32 * q : 32 * q + 4, :].bitcast(I32),
-                    rows[src : src + 4, 0 : widths[a]].bitcast(I32),
-                )
+        for r in range(4):
+            nc.sync.dma_start(moved_sc[r:P:32, :].bitcast(I32), picked_sc[16 + r : P : 32, :].bitcast(I32))
+        wg_raw.append(load_gate_rows(1))
+        planes = (picked_sc, moved_sc)
 
         wu_codes = keep.tile([P, PASSES, R], I32, name="wu_codes", align_bytes=64)
-        for a in range(PASSES):
+        wu_sc = keep.tile([P, PASSES, R], U8, name="wu_sc", align_bytes=64)
+
+        def order_up(a):
             nc.vector.tensor_copy(
                 wu_codes[:, a, :].rearrange("p (t m) -> p m t", t=PACK),
-                wu_raw[:, a, :].rearrange("p (m t) -> p m t", t=PACK),
+                wu_raw[a][:].rearrange("p (m t) -> p m t", t=PACK),
             )
 
         moving = {}
-        for j0, n in PIECES:
-            both = keep.tile([P, n], U32, name=f"both{j0}", align_bytes=64)
+
+        def pick(j0, n):
+            both = keep.tile([P, n], U32, name=f"both{j0}", tag=BOTH_TAGS[j0], align_bytes=64)
             nc.vector.tensor_copy(both[:], tab[:].bitcast(U32).indirect(offsets[:, j0 // 16 : (j0 + n) // 16]))
             parted = keep.tile([P, PASSES, n], U16, name=f"parted{j0}", align_bytes=64)
             nc.vector.tensor_copy(parted[:], both[:].bitcast(U16).rearrange("p (j a) -> p a j", a=PASSES))
@@ -100,10 +99,22 @@ def tile_list_gmlpt_sigm_bias_kernel(
                 for a in range(PASSES):
                     moving[c, a] = parted[:, a, c * CHUNK - j0 : (c + 1) * CHUNK - j0].bitcast(FP4X4)
 
+        pick(0, 256)
+        order_up(0)
+        for a in range(PASSES):
+            nc.vector.tensor_copy(
+                wu_sc[:, a, :].rearrange("p (t m) -> p t m", t=PACK),
+                wu_sc_raw[:, a, :].rearrange("p (m t) -> p t m", t=PACK),
+            )
+        pick(256, 256)
+        order_up(1)
+        pick(512, 256)
+
+
         def bank(i, name):
             return psum.tile([P, 512], F32, name=name, tag=f"bank{i}")
 
-        def first_stage(acc, codes, scales, c, a):
+        def first_stage(acc, codes, scales, c, a, opens):
             for t in range(PACK):
                 nc.tensor.matmul_mx(
                     out=acc[:, t * CHUNK : (t + 1) * CHUNK],
@@ -111,69 +122,92 @@ def tile_list_gmlpt_sigm_bias_kernel(
                     lhsT_scale=scales[:, t * P : (t + 1) * P],
                     rhs=moving[c, a],
                     rhs_scale=planes[a][:, c * CHUNK : (c + 1) * CHUNK],
-                    start=(a == 0 and t == 0),
-                    stop=(a == PASSES - 1 and t == PACK - 1),
+                    start=(opens and t == 0),
+                    stop=(not opens and t == PACK - 1),
                 )
 
         up, gate = {}, {}
 
-        def up_pass(c, a):
-            first_stage(up[c], wu_codes[:, a, :], planes[a][:, J : J + R], c, a)
+        def up_pass(c, a, opens):
+            first_stage(up[c], wu_codes[:, a, :], wu_sc[:, a, :], c, a, opens)
 
         def gate_pass(c, a):
-            first_stage(gate[c], wg_codes[a], wg_sc[a], c, a)
+            first_stage(gate[c], wg_codes[a], wg_sc[a], c, a, a == 0)
 
         for c in range(EARLY_UP):
             up[c] = bank(c, f"up{c}")
-        for c in range(4):
-            up_pass(c, 0)
-        for c in range(4):
-            up_pass(c, 1)
+        for a in range(PASSES):
+            for c in range(4):
+                up_pass(c, a, a == 0)
         for c in range(4, EARLY_UP):
-            up_pass(c, 0)
-            up_pass(c, 1)
+            up_pass(c, 1, True)
+            up_pass(c, 0, False)
+
+        up_view = {c: up[c][:].rearrange("p (t j) -> p j t", t=PACK) for c in range(EARLY_UP)}
 
         wg_codes, wg_sc = [], []
         for a in range(PASSES):
-            woven = keep.tile([P, PACK * R], BF16, name=f"wg_woven{a}", align_bytes=64)
-            dst = woven[:].rearrange("p (t m i) -> p m t i", t=PACK, i=PACK)
-            src = wg_raw[a][:].rearrange("p i (m t) -> p m t i", t=PACK)
+            woven = keep.tile([P, PACK * R], BF16, name=f"wg_woven{a}", tag=f"woven{a}", align_bytes=64)
+            dst = woven[:].rearrange("p (t m i) -> p m i t", t=PACK, i=PACK)
+            src = wg_raw[a][:].rearrange("p i (m t) -> p m i t", t=PACK)
             cut = SCALAR_M[a]
             nc.scalar.copy(dst[:, 0:cut], src[:, 0:cut])
-            nc.vector.tensor_copy(dst[:, cut:P], src[:, cut:P])
+            if cut < P:
+                nc.vector.tensor_copy(dst[:, cut:P], src[:, cut:P])
             codes = keep.tile([P, R], U32, name=f"wg_codes{a}", align_bytes=64)
             scales = keep.tile([P, R], U8, name=f"wg_sc{a}", align_bytes=64)
-            nc.vector.quantize_mx(out=codes[:].bitcast(FP8X4), scales=scales[:], in_=woven[:])
+            parts = 1 + a
+            for part in range(parts):
+                c0, c1 = part * R // parts, (part + 1) * R // parts
+                nc.vector.quantize_mx(
+                    out=codes[:, c0:c1].bitcast(FP8X4), scales=scales[:, c0:c1], in_=woven[:, PACK * c0 : PACK * c1]
+                )
             wg_codes.append(codes[:])
             wg_sc.append(scales[:])
 
-        wd = keep.tile([P, 2 * N], U8, name="wd", tag="stage0", align_bytes=64)
+        parked = keep.tile([P, 2, CHUNK, PACK], F32, name="parked", tag="stage1", align_bytes=64)
+        for c in range(2):
+            nc.scalar.copy(parked[:, c], up_view[c])
+            up_view[c] = parked[:, c]
+
+        wd = keep.tile([P, 2 * N], U8, name="wd", align_bytes=64)
         nc.sync.dma_start(wd[:].bitcast(I32), wd_words[0].bitcast(I32))
-        bias = keep.tile([P, N // P], F32, name="bias", tag="stage1", align_bytes=64)
+        wd_sc = keep.tile([P, N], U8, name="wd_sc", align_bytes=64)
+        nc.vector.memset(wd_sc[:].bitcast(I32), 0)
+        for q in range(4):
+            nc.sync.dma_start(
+                wd_sc[32 * q : 32 * q + 4, :].bitcast(I32), wd_scales[0, 4 * q : 4 * q + 4, :].bitcast(I32)
+            )
+        bias = keep.tile([P, N // P], F32, name="bias")
         with nc.allow_non_contiguous_dma(reason="one bias value a partition and row tile"):
             nc.sync.dma_start(bias[:], b.rearrange("(i p) -> p i", p=P))
+        pick(768, 256)
 
         hidden, quantised = {}, {}
 
         def sigmoid(c):
-            s = ring.tile([P, CHUNK, PACK], F32, name="sig")
+            s = keep.tile([P, CHUNK, PACK], F32, name=f"sig{c}")
             nc.scalar.activation(s[:], gate[c][:].rearrange("p (t j) -> p j t", t=PACK), ACT.Sigmoid)
             return s
 
+        group_of = {c: g for g, chunks in enumerate(GROUPS) for c in chunks}
+
         def product(c, s):
-            g, half = divmod(c, GROUP // CHUNK)
-            if half == 0:
-                hidden[g] = ring.tile([P, GROUP, PACK], BF16, name="hidden", align_bytes=64)
+            g = group_of[c]
+            place = c - GROUPS[g][0]
+            if place == 0:
+                hidden[g] = ring.tile([P, len(GROUPS[g]) * CHUNK, PACK], BF16, name="hidden", align_bytes=64)
             nc.vector.tensor_tensor(
-                hidden[g][:, half * CHUNK : (half + 1) * CHUNK, :],
-                up[c][:].rearrange("p (t j) -> p j t", t=PACK),
+                hidden[g][:, place * CHUNK : (place + 1) * CHUNK, :],
+                up_view[c],
                 s[:],
                 ALU.mult,
             )
 
         def quantise(g):
-            codes = ring.tile([P, GROUP], U32, name="h_codes", align_bytes=64)
-            scales = ring.tile([P, GROUP], U8, name="h_sc", align_bytes=64)
+            width = len(GROUPS[g]) * CHUNK
+            codes = ring.tile([P, width], U32, name="h_codes", align_bytes=64)
+            scales = ring.tile([P, width], U8, name="h_sc", align_bytes=64)
             nc.vector.quantize_mx(
                 out=codes[:].bitcast(FP8X4), scales=scales[:], in_=hidden[g][:].rearrange("p j t -> p (j t)")
             )
@@ -181,69 +215,88 @@ def tile_list_gmlpt_sigm_bias_kernel(
 
         out_tiles = out.rearrange("(i p) j -> p i j", p=P)
 
+        down = {}
+
         def second_stage(g, banks):
             codes, scales = quantised[g]
+            width = len(GROUPS[g]) * CHUNK
             for pair in range(2):
                 acc = bank(banks[pair], f"down{g}_{pair}")
-                res = ring.tile([P, 2, GROUP], F32, name=f"res{pair}")
+                down[g, pair] = acc
                 for e in range(2):
                     i = 2 * pair + e
                     nc.tensor.matmul_mx(
-                        out=acc[:, e * GROUP : (e + 1) * GROUP],
+                        out=acc[:, e * width : (e + 1) * width],
                         lhsT=wd[:, 2 * P * i : 2 * P * (i + 1)].bitcast(FP4X4),
-                        lhsT_scale=planes[0][:, J + R + P * i : J + R + P * (i + 1)],
+                        lhsT_scale=wd_sc[:, P * i : P * (i + 1)],
                         rhs=codes[:].bitcast(FP8X4),
                         rhs_scale=scales[:],
                         start=True,
                         stop=True,
                     )
-                for e in range(2):
-                    i = 2 * pair + e
-                    if pair == 0 or g == 0:
-                        nc.scalar.activation(
-                            res[:, e, :], acc[:, e * GROUP : (e + 1) * GROUP], ACT.Identity, bias=bias[:, i : i + 1]
-                        )
-                    else:
-                        nc.vector.tensor_scalar_add(res[:, e, :], acc[:, e * GROUP : (e + 1) * GROUP], bias[:, i : i + 1])
-                nc.sync.dma_start(out_tiles[:, 2 * pair : 2 * pair + 2, g * GROUP : (g + 1) * GROUP], res[:])
+
+        def finish(g, pair):
+            width = len(GROUPS[g]) * CHUNK
+            j0 = GROUPS[g][0] * CHUNK
+            res = ring.tile([P, 2, width], F32, name=f"res{pair}")
+            for e in range(2):
+                i = 2 * pair + e
+                sums = down[g, pair][:, e * width : (e + 1) * width]
+                if pair == 0 or g in SCALAR_GROUPS:
+                    nc.scalar.activation(res[:, e, :], sums, ACT.Identity, bias=bias[:, i : i + 1])
+                else:
+                    nc.vector.tensor_scalar_add(res[:, e, :], sums, bias[:, i : i + 1])
+            nc.sync.dma_start(out_tiles[:, 2 * pair : 2 * pair + 2, j0 : j0 + width], res[:])
 
         sigs = {}
 
         def gate_chunk(c, passes):
             if 0 in passes:
-                gate[c] = bank(6 + c % 2, f"gate{c}")
+                gate[c] = bank(GATE_BANKS[c % 4], f"gate{c}")
             for a in passes:
                 gate_pass(c, a)
             if 1 in passes:
                 sigs[c] = sigmoid(c)
 
-        gate_chunk(0, (0,))
-        gate_chunk(1, (0,))
-        gate_chunk(0, (1,))
-        gate_chunk(1, (1,))
-        product(0, sigs[0])
+        def late_up(c):
+            up[c] = bank(c, f"up{c}")
+            up_pass(c, 0, True)
+            up_pass(c, 1, False)
+            up_view[c] = up[c][:].rearrange("p (t j) -> p j t", t=PACK)
+
+        for a in range(PASSES):
+            for c in range(2):
+                gate_chunk(c, (a,))
         gate_chunk(2, (0, 1))
-        product(1, sigs[1])
         gate_chunk(3, (0, 1))
+        product(0, sigs[0])
+        gate_chunk(4, (0, 1))
+        product(1, sigs[1])
+        gate_chunk(5, (0, 1))
         product(2, sigs[2])
         quantise(0)
-        second_stage(0, (0, 1))
-        gate_chunk(4, (0, 1))
         product(3, sigs[3])
-        gate_chunk(5, (0, 1))
+        second_stage(0, (2, 3))
+        finish(0, 0)
+        finish(0, 1)
+        gate_chunk(6, (0, 1))
+        gate_chunk(7, (0, 1))
         product(4, sigs[4])
         quantise(1)
-        second_stage(1, (0, 1))
-        gate_chunk(6, (0, 1))
+        second_stage(1, (2, 3))
+        finish(1, 0)
+        finish(1, 1)
+        late_up(6)
+        late_up(7)
         product(5, sigs[5])
-        gate_chunk(7, (0, 1))
-        for c in (6, 7):
-            up[c] = bank(c - 4, f"up{c}")
-            up_pass(c, 0)
-            up_pass(c, 1)
-        quantise(2)
         product(6, sigs[6])
-        product(7, sigs[7])
+        quantise(2)
         second_stage(2, (4, 5))
         quantise(3)
         second_stage(3, (0, 1))
+        product(7, sigs[7])
+        quantise(4)
+        second_stage(4, (2, 3))
+        for g in range(2, len(GROUPS)):
+            finish(g, 0)
+            finish(g, 1)

@@ -21,10 +21,9 @@ PACK = 4
 PASSES = K // (P * PACK)
 CHUNK = 128
 SCALAR_M = (128, 44)
-GROUPS = ((0, 1), (2, 3), (4, 5), (6,), (7,))
+GROUPS = ((0,), (1,), (2, 3), (4, 5), (6,), (7,))
 EARLY_UP = 6
-SCALAR_GROUPS = (1, 2)
-GATE_BANKS = (6, 7, 0, 1)
+SCALAR_GROUPS = (0, 1, 2)
 BOTH_TAGS = {0: "both0", 256: "both256", 512: "wu_raw1", 768: "woven1"}
 
 
@@ -35,7 +34,7 @@ def tile_list_gmlpt_sigm_bias_kernel(
     with ExitStack() as ctx:
         keep = ctx.enter_context(tc.tile_pool(name="keep", bufs=1))
         ring = ctx.enter_context(tc.tile_pool(name="ring", bufs=4))
-        psum = ctx.enter_context(tc.psum_pool(name="psum", bufs=1))
+        psum = ctx.enter_context(tc.psum_pool(name="psum", bufs=8))
 
         offsets = keep.tile([P, J // 16], U16, name="offsets")
         nc.sync.dma_start(offsets[:], offs)
@@ -111,8 +110,8 @@ def tile_list_gmlpt_sigm_bias_kernel(
         pick(512, 256)
 
 
-        def bank(i, name):
-            return psum.tile([P, 512], F32, name=name, tag=f"bank{i}")
+        def bank(name):
+            return psum.tile([P, 512], F32, name=name, tag="bank")
 
         def first_stage(acc, codes, scales, c, a, opens):
             for t in range(PACK):
@@ -135,7 +134,7 @@ def tile_list_gmlpt_sigm_bias_kernel(
             first_stage(gate[c], wg_codes[a], wg_sc[a], c, a, a == 0)
 
         for c in range(EARLY_UP):
-            up[c] = bank(c, f"up{c}")
+            up[c] = bank(f"up{c}")
         for a in range(PASSES):
             for c in range(4):
                 up_pass(c, a, a == 0)
@@ -217,11 +216,11 @@ def tile_list_gmlpt_sigm_bias_kernel(
 
         down = {}
 
-        def second_stage(g, banks):
+        def second_stage(g):
             codes, scales = quantised[g]
             width = len(GROUPS[g]) * CHUNK
             for pair in range(2):
-                acc = bank(banks[pair], f"down{g}_{pair}")
+                acc = bank(f"down{g}_{pair}")
                 down[g, pair] = acc
                 for e in range(2):
                     i = 2 * pair + e
@@ -252,14 +251,14 @@ def tile_list_gmlpt_sigm_bias_kernel(
 
         def gate_chunk(c, passes):
             if 0 in passes:
-                gate[c] = bank(GATE_BANKS[c % 4], f"gate{c}")
+                gate[c] = bank(f"gate{c}")
             for a in passes:
                 gate_pass(c, a)
             if 1 in passes:
                 sigs[c] = sigmoid(c)
 
         def late_up(c):
-            up[c] = bank(c, f"up{c}")
+            up[c] = bank(f"up{c}")
             up_pass(c, 0, True)
             up_pass(c, 1, False)
             up_view[c] = up[c][:].rearrange("p (t j) -> p j t", t=PACK)
@@ -272,31 +271,35 @@ def tile_list_gmlpt_sigm_bias_kernel(
         product(0, sigs[0])
         gate_chunk(4, (0, 1))
         product(1, sigs[1])
-        gate_chunk(5, (0, 1))
-        product(2, sigs[2])
         quantise(0)
-        product(3, sigs[3])
-        second_stage(0, (2, 3))
+        second_stage(0)
         finish(0, 0)
         finish(0, 1)
-        gate_chunk(6, (0, 1))
-        gate_chunk(7, (0, 1))
-        product(4, sigs[4])
+        product(2, sigs[2])
         quantise(1)
-        second_stage(1, (2, 3))
+        gate_chunk(5, (0, 1))
+        second_stage(1)
         finish(1, 0)
         finish(1, 1)
+        product(3, sigs[3])
+        gate_chunk(6, (0, 1))
+        product(4, sigs[4])
+        quantise(2)
+        gate_chunk(7, (0, 1))
+        second_stage(2)
+        finish(2, 0)
+        finish(2, 1)
         late_up(6)
         late_up(7)
         product(5, sigs[5])
         product(6, sigs[6])
-        quantise(2)
-        second_stage(2, (4, 5))
         quantise(3)
-        second_stage(3, (0, 1))
-        product(7, sigs[7])
+        second_stage(3)
         quantise(4)
-        second_stage(4, (2, 3))
-        for g in range(2, len(GROUPS)):
+        second_stage(4)
+        product(7, sigs[7])
+        quantise(5)
+        second_stage(5)
+        for g in range(3, len(GROUPS)):
             finish(g, 0)
             finish(g, 1)

@@ -20,7 +20,7 @@ P = 128
 PACK = 4
 PASSES = K // (P * PACK)
 CHUNK = 128
-SCALAR_M = (128, 44)
+SCALAR_M = (96, 44)
 GROUPS = ((0,), (1,), (2, 3), (4, 5), (6,), (7,))
 EARLY_UP = 6
 SCALAR_GROUPS = (0, 1, 2)
@@ -151,8 +151,7 @@ def tile_list_gmlpt_sigm_bias_kernel(
             src = wg_raw[a][:].rearrange("p i (m t) -> p m i t", t=PACK)
             cut = SCALAR_M[a]
             nc.scalar.copy(dst[:, 0:cut], src[:, 0:cut])
-            if cut < P:
-                nc.vector.tensor_copy(dst[:, cut:P], src[:, cut:P])
+            nc.vector.tensor_copy(dst[:, cut:P], src[:, cut:P])
             codes = keep.tile([P, R], U32, name=f"wg_codes{a}", align_bytes=64)
             scales = keep.tile([P, R], U8, name=f"wg_sc{a}", align_bytes=64)
             parts = 1 + a

from contextlib import ExitStack

import concourse.mybir as mybir

K, R, N, T, J = 1024, 512, 512, 2048, 1024
FLOPS = 2 * J * (2 * K * R + R * N)

F32 = mybir.dt.float32
BF16 = mybir.dt.bfloat16
I32 = mybir.dt.int32
U32 = mybir.dt.uint32
U16 = mybir.dt.uint16
U8 = mybir.dt.uint8
FP8X4 = mybir.dt.float8_e4m3fn_x4
FP4X4 = mybir.dt.float4_e2m1fn_x4
ACT = mybir.ActivationFunctionType
ALU = mybir.AluOpType

P = 128
PACK = 4
PASSES = K // (P * PACK)
CHUNK = 128
SCALAR_M = (96, 44)
GROUPS = ((0,), (1,), (2, 3), (4, 5), (6,), (7,))
EARLY_UP = 6
SCALAR_GROUPS = (0, 1, 2)
BOTH_TAGS = {0: "both0", 256: "both256", 512: "wu_raw1", 768: "woven1"}


def tile_list_gmlpt_sigm_bias_kernel(
    tc, tab_words, tab_scales, wg, wu_words, wu_scales, wd_words, wd_scales, b, offs, out
):
    nc = tc.nc
    with ExitStack() as ctx:
        keep = ctx.enter_context(tc.tile_pool(name="keep", bufs=1))
        ring = ctx.enter_context(tc.tile_pool(name="ring", bufs=4))
        psum = ctx.enter_context(tc.psum_pool(name="psum", bufs=8))

        offsets = keep.tile([P, J // 16], U16, name="offsets")
        nc.sync.dma_start(offsets[:], offs)

        def load_up_words(a):
            raw = keep.tile([P, R], I32, name=f"wu_raw{a}", tag=f"wu_raw{a}", align_bytes=64)
            nc.sync.dma_start(raw[:], wu_words[a].rearrange("p r i -> p (r i)").bitcast(I32))
            return raw

        def load_gate_rows(a):
            raw = keep.tile([P, PACK, R], F32, name=f"wg_raw{a}", tag=f"stage{a}", align_bytes=64)
            nc.sync.dma_start(raw[:], wg[512 * a : 512 * (a + 1), :].rearrange("(p i) r -> p i r", i=PACK))
            return raw

        wu_raw = [load_up_words(0)]
        tab_sc = keep.tile([P, T], U8, name="tab_sc", align_bytes=64)
        nc.vector.memset(tab_sc[:].bitcast(I32), 0)
        tab_rows = tab_scales.rearrange("a (q r) t -> r q a t", r=4).bitcast(I32)
        for r in range(4):
            nc.sync.dma_start(tab_sc[r:P:16, :].bitcast(I32), tab_rows[r])
        tab = keep.tile([P, T], I32, name="tab", align_bytes=64)
        nc.sync.dma_start(tab[:], tab_words[0].rearrange("p t i -> p (t i)").bitcast(I32))
        wu_sc_raw = keep.tile([P, PASSES, R], U8, name="wu_sc_raw", tag="both256", align_bytes=64)
        nc.vector.memset(wu_sc_raw[:].bitcast(I32), 0)
        wu_rows = wu_scales.rearrange("a (q r) n -> q r a n", r=4).bitcast(I32)
        for q in range(4):
            nc.sync.dma_start(wu_sc_raw[32 * q : 32 * q + 4, :, :].bitcast(I32), wu_rows[q])
        wu_raw.append(load_up_words(1))
        wg_raw = [load_gate_rows(0)]

        warm = keep.tile([P, 2], F32, name="warm")
        nc.vector.memset(warm[:, 0:1], 0.0)
        nc.scalar.activation(warm[:, 1:2], warm[:, 0:1], ACT.Sigmoid)

        picked_sc = keep.tile([P, J], U8, name="picked_sc", align_bytes=64)
        moved_sc = keep.tile([P, J], U8, name="moved_sc", align_bytes=64)
        nc.vector.memset(moved_sc[:].bitcast(I32), 0)
        nc.vector.tensor_copy(picked_sc[:], tab_sc[:].indirect(offsets[:]))
        for r in range(4):
            nc.sync.dma_start(moved_sc[r:P:32, :].bitcast(I32), picked_sc[16 + r : P : 32, :].bitcast(I32))
        wg_raw.append(load_gate_rows(1))
        planes = (picked_sc, moved_sc)

        wu_codes = keep.tile([P, PASSES, R], I32, name="wu_codes", align_bytes=64)
        wu_sc = keep.tile([P, PASSES, R], U8, name="wu_sc", align_bytes=64)

        def order_up(a):
            nc.vector.tensor_copy(
                wu_codes[:, a, :].rearrange("p (t m) -> p m t", t=PACK),
                wu_raw[a][:].rearrange("p (m t) -> p m t", t=PACK),
            )

        moving = {}

        def pick(j0, n):
            both = keep.tile([P, n], U32, name=f"both{j0}", tag=BOTH_TAGS[j0], align_bytes=64)
            nc.vector.tensor_copy(both[:], tab[:].bitcast(U32).indirect(offsets[:, j0 // 16 : (j0 + n) // 16]))
            parted = keep.tile([P, PASSES, n], U16, name=f"parted{j0}", align_bytes=64)
            nc.vector.tensor_copy(parted[:], both[:].bitcast(U16).rearrange("p (j a) -> p a j", a=PASSES))
            for c in range(j0 // CHUNK, (j0 + n) // CHUNK):
                for a in range(PASSES):
                    moving[c, a] = parted[:, a, c * CHUNK - j0 : (c + 1) * CHUNK - j0].bitcast(FP4X4)

        pick(0, 256)
        order_up(0)
        for a in range(PASSES):
            nc.vector.tensor_copy(
                wu_sc[:, a, :].rearrange("p (t m) -> p t m", t=PACK),
                wu_sc_raw[:, a, :].rearrange("p (m t) -> p t m", t=PACK),
            )
        pick(256, 256)
        order_up(1)
        pick(512, 256)


        def bank(name):
            return psum.tile([P, 512], F32, name=name, tag="bank")

        def first_stage(acc, codes, scales, c, a, opens):
            for t in range(PACK):
                nc.tensor.matmul_mx(
                    out=acc[:, t * CHUNK : (t + 1) * CHUNK],
                    lhsT=codes[:, t * P : (t + 1) * P].bitcast(FP8X4),
                    lhsT_scale=scales[:, t * P : (t + 1) * P],
                    rhs=moving[c, a],
                    rhs_scale=planes[a][:, c * CHUNK : (c + 1) * CHUNK],
                    start=(opens and t == 0),
                    stop=(not opens and t == PACK - 1),
                )

        up, gate = {}, {}

        def up_pass(c, a, opens):
            first_stage(up[c], wu_codes[:, a, :], wu_sc[:, a, :], c, a, opens)

        def gate_pass(c, a):
            first_stage(gate[c], wg_codes[a], wg_sc[a], c, a, a == 0)

        for c in range(EARLY_UP):
            up[c] = bank(f"up{c}")
        for a in range(PASSES):
            for c in range(4):
                up_pass(c, a, a == 0)
        for c in range(4, EARLY_UP):
            up_pass(c, 1, True)
            up_pass(c, 0, False)

        up_view = {c: up[c][:].rearrange("p (t j) -> p j t", t=PACK) for c in range(EARLY_UP)}

        wg_codes, wg_sc = [], []
        for a in range(PASSES):
            woven = keep.tile([P, PACK * R], BF16, name=f"wg_woven{a}", tag=f"woven{a}", align_bytes=64)
            dst = woven[:].rearrange("p (t m i) -> p m i t", t=PACK, i=PACK)
            src = wg_raw[a][:].rearrange("p i (m t) -> p m i t", t=PACK)
            cut = SCALAR_M[a]
            nc.scalar.copy(dst[:, 0:cut], src[:, 0:cut])
            nc.vector.tensor_copy(dst[:, cut:P], src[:, cut:P])
            codes = keep.tile([P, R], U32, name=f"wg_codes{a}", align_bytes=64)
            scales = keep.tile([P, R], U8, name=f"wg_sc{a}", align_bytes=64)
            parts = 1 + a
            for part in range(parts):
                c0, c1 = part * R // parts, (part + 1) * R // parts
                nc.vector.quantize_mx(
                    out=codes[:, c0:c1].bitcast(FP8X4), scales=scales[:, c0:c1], in_=woven[:, PACK * c0 : PACK * c1]
                )
            wg_codes.append(codes[:])
            wg_sc.append(scales[:])

        parked = keep.tile([P, 2, CHUNK, PACK], F32, name="parked", tag="stage1", align_bytes=64)
        for c in range(2):
            nc.scalar.copy(parked[:, c], up_view[c])
            up_view[c] = parked[:, c]

        wd = keep.tile([P, 2 * N], U8, name="wd", align_bytes=64)
        nc.sync.dma_start(wd[:].bitcast(I32), wd_words[0].bitcast(I32))
        wd_sc = keep.tile([P, N], U8, name="wd_sc", align_bytes=64)
        nc.vector.memset(wd_sc[:].bitcast(I32), 0)
        for q in range(4):
            nc.sync.dma_start(
                wd_sc[32 * q : 32 * q + 4, :].bitcast(I32), wd_scales[0, 4 * q : 4 * q + 4, :].bitcast(I32)
            )
        bias = keep.tile([P, N // P], F32, name="bias")
        with nc.allow_non_contiguous_dma(reason="one bias value a partition and row tile"):
            nc.sync.dma_start(bias[:], b.rearrange("(i p) -> p i", p=P))
        pick(768, 256)

        hidden, quantised = {}, {}

        def sigmoid(c):
            s = keep.tile([P, CHUNK, PACK], F32, name=f"sig{c}")
            nc.scalar.activation(s[:], gate[c][:].rearrange("p (t j) -> p j t", t=PACK), ACT.Sigmoid)
            return s

        group_of = {c: g for g, chunks in enumerate(GROUPS) for c in chunks}

        def product(c, s):
            g = group_of[c]
            place = c - GROUPS[g][0]
            if place == 0:
                hidden[g] = ring.tile([P, len(GROUPS[g]) * CHUNK, PACK], BF16, name="hidden", align_bytes=64)
            nc.vector.tensor_tensor(
                hidden[g][:, place * CHUNK : (place + 1) * CHUNK, :],
                up_view[c],
                s[:],
                ALU.mult,
            )

        def quantise(g):
            width = len(GROUPS[g]) * CHUNK
            codes = ring.tile([P, width], U32, name="h_codes", align_bytes=64)
            scales = ring.tile([P, width], U8, name="h_sc", align_bytes=64)
            nc.vector.quantize_mx(
                out=codes[:].bitcast(FP8X4), scales=scales[:], in_=hidden[g][:].rearrange("p j t -> p (j t)")
            )
            quantised[g] = (codes, scales)

        out_tiles = out.rearrange("(i p) j -> p i j", p=P)

        down = {}

        def second_stage(g):
            codes, scales = quantised[g]
            width = len(GROUPS[g]) * CHUNK
            for pair in range(2):
                acc = bank(f"down{g}_{pair}")
                down[g, pair] = acc
                for e in range(2):
                    i = 2 * pair + e
                    nc.tensor.matmul_mx(
                        out=acc[:, e * width : (e + 1) * width],
                        lhsT=wd[:, 2 * P * i : 2 * P * (i + 1)].bitcast(FP4X4),
                        lhsT_scale=wd_sc[:, P * i : P * (i + 1)],
                        rhs=codes[:].bitcast(FP8X4),
                        rhs_scale=scales[:],
                        start=True,
                        stop=True,
                    )

        def finish(g, pair):
            width = len(GROUPS[g]) * CHUNK
            j0 = GROUPS[g][0] * CHUNK
            res = ring.tile([P, 2, width], F32, name=f"res{pair}")
            for e in range(2):
                i = 2 * pair + e
                sums = down[g, pair][:, e * width : (e + 1) * width]
                if pair == 0 or g in SCALAR_GROUPS:
                    nc.scalar.activation(res[:, e, :], sums, ACT.Identity, bias=bias[:, i : i + 1])
                else:
                    nc.vector.tensor_scalar_add(res[:, e, :], sums, bias[:, i : i + 1])
            nc.sync.dma_start(out_tiles[:, 2 * pair : 2 * pair + 2, j0 : j0 + width], res[:])

        sigs = {}

        def gate_chunk(c, passes):
            if 0 in passes:
                gate[c] = bank(f"gate{c}")
            for a in passes:
                gate_pass(c, a)
            if 1 in passes:
                sigs[c] = sigmoid(c)

        def late_up(c):
            up[c] = bank(f"up{c}")
            up_pass(c, 0, True)
            up_pass(c, 1, False)
            up_view[c] = up[c][:].rearrange("p (t j) -> p j t", t=PACK)

        for a in range(PASSES):
            for c in range(2):
                gate_chunk(c, (a,))
        gate_chunk(2, (0, 1))
        gate_chunk(3, (0, 1))
        product(0, sigs[0])
        gate_chunk(4, (0, 1))
        product(1, sigs[1])
        quantise(0)
        second_stage(0)
        finish(0, 0)
        finish(0, 1)
        product(2, sigs[2])
        quantise(1)
        gate_chunk(5, (0, 1))
        second_stage(1)
        finish(1, 0)
        finish(1, 1)
        product(3, sigs[3])
        gate_chunk(6, (0, 1))
        product(4, sigs[4])
        quantise(2)
        gate_chunk(7, (0, 1))
        second_stage(2)
        finish(2, 0)
        finish(2, 1)
        late_up(6)
        late_up(7)
        product(5, sigs[5])
        product(6, sigs[6])
        quantise(3)
        second_stage(3)
        quantise(4)
        second_stage(4)
        product(7, sigs[7])
        quantise(5)
        second_stage(5)
        for g in range(3, len(GROUPS)):
            finish(g, 0)
            finish(g, 1)
